import numpy as np
import ml_dtypes


def mxq(x, axis, fmt="e4m3"):
    dtype, down = {"e4m3": (ml_dtypes.float8_e4m3fn, 7), "e5m2": (ml_dtypes.float8_e5m2, 14)}[fmt]
    v = np.moveaxis(np.asarray(x, np.float32).astype(ml_dtypes.bfloat16).astype(np.float64), axis, -1)
    blocks = v.reshape(v.shape[:-1] + (-1, 32))
    amax = np.abs(blocks).max(-1, keepdims=True)
    byte = np.maximum(np.where(amax > 0, np.frexp(amax)[1] - 1 + 127, 0) - down, 1)
    scale = np.exp2(byte - 127.0)
    codes = (blocks / scale).astype(np.float32).astype(dtype).astype(np.float64)
    return np.moveaxis((codes * scale).reshape(v.shape), -1, axis)


WIDE = False


def mx_kscale(k):
    if not WIDE:
        return np.ones(k)
    levels = np.array([10, -10, 5, -5, 0])
    if k % 512:
        return np.exp2(np.random.permutation(np.resize(levels, k // 32))).repeat(32)
    a = np.empty((k // 512, 16))
    for p in range(k // 512):
        a[p, :8] = np.random.permutation(np.resize(levels, 8))
        for g in range(8):
            far = levels[np.abs(levels - a[p, g]) >= 10]
            a[p, g + 8] = far[np.random.randint(len(far))]
    return np.exp2(a.ravel()).repeat(32)


def f64(x):
    return np.asarray(x).astype(np.float64)


def striped(idx):
    return np.tile(idx.reshape(-1, 16).T, (8, 1)).astype(np.uint16)


def unstriped(offs):
    return offs[:16].T.reshape(-1).astype(np.int64)


E2M1 = np.array([0.0, 0.5, 1.0, 1.5, 2.0, 3.0, 4.0, 6.0, -0.0, -0.5, -1.0, -1.5, -2.0, -3.0, -4.0, -6.0])


def pack_weight(w, fmt):
    k, n = w.shape
    w = f64(np.asarray(w, np.float32).astype(ml_dtypes.bfloat16)).reshape(k // 32, 32, n)
    amax = np.abs(w).max(1)
    if fmt == "e4m3":
        byte = np.frexp(amax)[1] - 1 + 127 - 7
    else:
        mant, ex = np.frexp(amax / 6.0)
        byte = np.where(mant > 0.5, ex, ex - 1) + 127
    byte = np.clip(np.where(amax > 0, byte, 1), 1, 254)
    scaled = (w * np.exp2(127.0 - byte)[:, None, :]).reshape(k, n).astype(np.float32)
    by_word = np.ascontiguousarray(scaled.reshape(k // 512, 128, 4, n).transpose(0, 1, 3, 2))
    if fmt == "e4m3":
        words = by_word.astype(ml_dtypes.float8_e4m3fn).view(np.uint8)
    else:
        c = by_word.astype(ml_dtypes.float4_e2m1fn).view(np.uint8) & 0xF
        words = (c[..., 0::2] | (c[..., 1::2] << 4)).reshape(k // 512, 128, 2 * n)
    return np.ascontiguousarray(words), np.ascontiguousarray(byte.astype(np.uint8).reshape(k // 512, 16, n))


def unpack_weight(words, scales, fmt):
    g, _, n = scales.shape
    words = np.ascontiguousarray(words).reshape(g, 128, n, -1)
    if fmt == "e4m3":
        vals = words.view(ml_dtypes.float8_e4m3fn).astype(np.float64)
    else:
        nib = np.empty((g, 128, n, 4), np.uint8)
        nib[..., 0::2] = words & 0xF
        nib[..., 1::2] = words >> 4
        vals = E2M1[nib]
    vals = vals * np.repeat(np.exp2(scales.astype(np.float64) - 127.0), 8, axis=1)[..., None]
    return vals.transpose(0, 1, 3, 2).reshape(g * 512, n)


def gelu(v):
    return 0.5 * v * (1.0 + np.tanh(np.sqrt(2.0 / np.pi) * (v + 0.044715 * v**3)))


K, L, T, Q, E, C, D = 512, 1024, 768, 1024, 2, 256, 256
H, N = 512, 128


def by_expert(wq, xq, C):
    return np.concatenate([wq[e].T @ xq[:, e * C:(e + 1) * C] for e in range(E)], axis=1)


def setup_inputs():
    n = np.random.standard_normal
    s = mx_kscale(K)
    v = mx_kscale(L)
    u = mx_kscale(H)
    slots1, slots2 = np.random.permutation(T)[:E * C], np.random.permutation(Q)[:E * D]
    x = pack_weight(n((K, T)) * s[:, None], "e4m3")
    z = pack_weight(n((L, Q)) * v[:, None], "e4m3")
    w1 = [pack_weight(m, "e2m1") for m in n((E, K, H)) / np.sqrt(K) / s[None, :, None] * u]
    wz = [pack_weight(m, "e2m1") for m in n((E, L, H)) / np.sqrt(L) / v[None, :, None] * u]
    w2 = [pack_weight(m, "e2m1") for m in n((E, H, N)) / np.sqrt(H) / u[None, :, None]]
    return {
        "x_words": x[0],
        "x_scales": x[1],
        "z_words": z[0],
        "z_scales": z[1],
        "w1_words": np.stack([m[0] for m in w1]),
        "w1_scales": np.stack([m[1] for m in w1]),
        "wz_words": np.stack([m[0] for m in wz]),
        "wz_scales": np.stack([m[1] for m in wz]),
        "w2_words": np.stack([m[0] for m in w2]),
        "w2_scales": np.stack([m[1] for m in w2]),
        "gate1": (np.tile(np.random.uniform(0.2, 1.0, E * C), (128, 1))).astype(np.float32),
        "gate2": (np.tile(np.random.uniform(0.2, 1.0, E * D), (128, 1))).astype(np.float32),
        "offs": striped(slots1),
        "offs2": striped(slots2),
    }


def reference(x_words, x_scales, z_words, z_scales, w1_words, w1_scales, wz_words, wz_scales, w2_words, w2_scales, gate1, gate2, offs, offs2):
    w1 = np.stack([unpack_weight(w1_words[e], w1_scales[e], "e2m1") for e in range(E)])
    wz = np.stack([unpack_weight(wz_words[e], wz_scales[e], "e2m1") for e in range(E)])
    w2 = np.stack([unpack_weight(w2_words[e], w2_scales[e], "e2m1") for e in range(E)])
    idx, idx2 = unstriped(offs), unstriped(offs2)
    xq = unpack_weight(x_words, x_scales, "e4m3")[:, idx]
    zq = unpack_weight(z_words, z_scales, "e4m3")[:, idx2]
    h = gelu(by_expert(w1, xq, C))
    p = gelu(by_expert(wz, zq, D))
    out = np.zeros((N, T + Q))
    out[:, idx] = f64(gate1[:1]) * by_expert(w2, mxq(h, 0, "e4m3"), C)
    out[:, T + idx2] = f64(gate2[:1]) * by_expert(w2, mxq(p, 0, "e4m3"), D)
    return out

@@ -1,0 +1,196 @@
+from contextlib import ExitStack
+
+import concourse.mybir as mybir
+from concourse.masks import make_identity
+
+F32 = mybir.dt.float32
+BF16 = mybir.dt.bfloat16
+I32 = mybir.dt.int32
+U32 = mybir.dt.uint32
+U16 = mybir.dt.uint16
+U8 = mybir.dt.uint8
+FP8X4 = mybir.dt.float8_e4m3fn_x4
+FP4X4 = mybir.dt.float4_e2m1fn_x4
+GELU = mybir.ActivationFunctionType.Gelu_apprx_tanh
+MULT = mybir.AluOpType.mult
+
+P = 128
+T, Q, E, C, H, N = 768, 1024, 2, 256, 512, 128
+FLOPS = 939524096
+
+
+def tile_moe_mmo_gelu_kernel(tc, x_words, x_scales, z_words, z_scales, w1_words, w1_scales, wz_words, wz_scales, w2_words, w2_scales, gate1, gate2, offs, offs2, out):
+    nc = tc.nc
+    with ExitStack() as ctx:
+        keep = ctx.enter_context(tc.tile_pool(name="keep", bufs=1))
+        ps1 = ctx.enter_context(tc.psum_pool(name="ps1", bufs=4))
+        pst = ctx.enter_context(tc.psum_pool(name="pst", bufs=2))
+        ps2 = ctx.enter_context(tc.psum_pool(name="ps2", bufs=2))
+
+        def tile(shape, dtype, name):
+            return keep.tile(shape, dtype, name=name, align_bytes=64)
+
+        list_x = keep.tile([P, E * C // 16], U16, name="list_x")
+        list_z = keep.tile([P, E * C // 16], U16, name="list_z")
+        xw = [tile([P, T], I32, "xw0")]
+        zw = [tile([P, Q], I32, "zw%d" % s) for s in range(2)]
+        xs = tile([P, 1, T], U8, "xs")
+        zs = tile([P, 2, Q], U8, "zs")
+        w1 = tile([P, 2, 2 * H], U8, "w1")
+        wz = tile([P, 4, 2 * H], U8, "wz")
+        w2 = tile([P, 2, 2 * N], U8, "w2")
+        w1s = tile([P, 2, H], U8, "w1s")
+        wzs = tile([P, 4, H], U8, "wzs")
+        w2s = tile([P, 2, N], U8, "w2s")
+        g1 = tile([P, E * C], F32, "g1")
+        g2 = tile([P, E * C], F32, "g2")
+        out_x = tile([P, T], F32, "out_x")
+        out_z = tile([P, Q], F32, "out_z")
+        ident = tile([P, P], F32, "ident")
+        warm_in = tile([P, 8], F32, "warm_in")
+        warm_out = tile([P, 8], F32, "warm_out")
+
+        def zero(plane, eng):
+            eng.memset(plane[:].rearrange("p a n -> p (a n)").bitcast(I32), 0)
+
+        def load_scales(plane, rows, eng):
+            for r in range(4):
+                eng.dma_start(out=plane[r:P:32, :, :].bitcast(I32), in_=rows[:, r:16:4, :].rearrange("a q n -> q a n").bitcast(I32))
+
+        def load_words(dst, words):
+            nc.sync.dma_start(out=dst[:], in_=words.rearrange("p t d -> p (t d)").bitcast(I32))
+
+        def load_weights(dst, words):
+            nc.sync.dma_start(out=dst[:].bitcast(I32), in_=words.rearrange("e s p n -> p (e s) n").bitcast(I32))
+
+        def merged(scales):
+            return scales.rearrange("e s b n -> (e s) b n")
+
+        zero(zs, nc.vector)
+        zero(wzs, nc.vector)
+        zero(xs, nc.vector)
+        zero(w1s, nc.vector)
+        nc.vector.memset(warm_in[:], 0.0)
+        nc.scalar.activation(warm_out[:], warm_in[:], GELU)
+        zero(w2s, nc.gpsimd)
+        load_scales(w2s, merged(w2_scales), nc.gpsimd)
+        make_identity(nc, ident[:])
+        nc.vector.memset(out_z[:], 0.0)
+        nc.vector.memset(out_x[:], 0.0)
+
+        nc.sync.dma_start(list_z[:], offs2)
+        load_words(zw[0], z_words[0])
+        load_scales(zs, z_scales, nc.sync)
+        load_words(zw[1], z_words[1])
+        load_weights(wz, wz_words)
+        load_scales(wzs, merged(wz_scales), nc.sync)
+        nc.sync.dma_start(list_x[:], offs)
+        load_words(xw[0], x_words[0])
+        load_scales(xs, x_scales, nc.sync)
+        load_weights(w1, w1_words)
+        load_scales(w1s, merged(w1_scales), nc.sync)
+        load_weights(w2, w2_words)
+        nc.sync.dma_start(out=g2[:], in_=gate2)
+        nc.sync.dma_start(out=g1[:], in_=gate1)
+
+        sides = {
+            "z": (list_z, zw, zs, wz, wzs, g2, out_z),
+            "x": (list_x, xw, xs, w1, w1s, g1, out_x),
+        }
+        units = [("z", 0), ("z", 1), ("x", 0), ("x", 1)]
+        words, scales, grouped, sums, gated = {}, {}, {}, {}, {}
+
+        def offsets(u):
+            side, e = units[u]
+            return sides[side][0][:, 16 * e : 16 * (e + 1)]
+
+        def gather_words(u, s):
+            words[u, s] = tile([P, C], U32, "gw%d_%d" % (u, s))
+            nc.vector.tensor_copy(words[u, s][:], sides[units[u][0]][1][s][:].bitcast(U32).indirect(offsets(u)))
+
+        def gather_scales(u, s):
+            scales[u, s] = tile([P, C], U8, "gs%d_%d" % (u, s))
+            nc.vector.tensor_copy(scales[u, s][:], sides[units[u][0]][2][:, s, :].indirect(offsets(u)))
+
+        def first_layer(u):
+            side, e = units[u]
+            w, ws = sides[side][3], sides[side][4]
+            passes = len(sides[side][1])
+            turned = pst.tile([P, 4, P], F32, name="turned")
+            hs = []
+            for j in range(2):
+                cols = slice(j * P, (j + 1) * P)
+                acc = ps1.tile([P, H], F32, name="acc")
+                for s in range(passes):
+                    nc.tensor.matmul_mx(
+                        out=acc[:],
+                        lhsT=words[u, s][:, cols].bitcast(FP8X4),
+                        lhsT_scale=scales[u, s][:, cols],
+                        rhs=w[:, e * passes + s, :].bitcast(FP4X4),
+                        rhs_scale=ws[:, e * passes + s, :],
+                        start=(s == 0),
+                        stop=(s == passes - 1),
+                    )
+                h = tile([P, H], BF16, "h%d_%d" % (u, j))
+                nc.scalar.activation(
+                    h[:].rearrange("s (v q b) -> s v q b", v=2, b=2),
+                    acc[:].rearrange("s (q v b) -> s v q b", v=2, b=2),
+                    GELU,
+                )
+                hs.append(h)
+            for j in range(2):
+                pairs = hs[j][:].bitcast(F32)
+                for v in range(2):
+                    nc.tensor.transpose(turned[:, 2 * j + v, :], pairs[:, v * P : (v + 1) * P], ident[:])
+            grouped[u] = tile([P, 4 * C], BF16, "grouped%d" % u)
+            nc.scalar.copy(
+                grouped[u][:].bitcast(F32).rearrange("q (j s v) -> q j s v", j=2, v=2),
+                turned[:].rearrange("q (j v) s -> q j s v", v=2),
+            )
+
+        def second_layer(u):
+            e = units[u][1]
+            codes = tile([P, C], U32, "codes%d" % u)
+            plane = tile([P, C], U8, "plane%d" % u)
+            nc.vector.quantize_mx(out=codes[:].bitcast(FP8X4), scales=plane[:], in_=grouped[u][:])
+            sums[u] = ps2.tile([P, C], F32, name="sums")
+            nc.tensor.matmul_mx(
+                out=sums[u][:],
+                lhsT=w2[:, e, :].bitcast(FP4X4),
+                lhsT_scale=w2s[:, e, :],
+                rhs=codes[:].bitcast(FP8X4),
+                rhs_scale=plane[:],
+                start=True,
+                stop=True,
+            )
+
+        def gate(u):
+            side, e = units[u]
+            gated[u] = tile([P, C], F32, "gated%d" % u)
+            nc.vector.tensor_tensor(gated[u][:], sums[u][:], sides[side][5][:, e * C : (e + 1) * C], MULT)
+
+        def scatter(u):
+            nc.vector.tensor_copy(sides[units[u][0]][6][:].indirect(offsets(u)), gated[u][:])
+
+        for u in range(2):
+            gather_words(u, 0)
+            gather_scales(u, 0)
+            gather_scales(u, 1)
+            gather_words(u, 1)
+            first_layer(u)
+        gather_words(2, 0)
+        gather_scales(2, 0)
+        first_layer(2)
+        gather_words(3, 0)
+        second_layer(0)
+        gather_scales(3, 0)
+        first_layer(3)
+        gate(0)
+        for u in range(1, 4):
+            second_layer(u)
+            scatter(u - 1)
+            if u == 2:
+                nc.sync.dma_start(out=out[:, T:], in_=out_z[:])
+            gate(u)
+        scatter(3)
+        nc.sync.dma_start(out=out[:, :T], in_=out_x[:])

@@ -61,35 +61,36 @@ def tile_moe_mmo_gelu_kernel(tc, x_words, x_scales, z_words, z_scales, w1_words,
             nc.sync.dma_start(out=dst[:], in_=words.rearrange("p t d -> p (t d)").bitcast(I32))
 
         def load_weights(dst, words):
-            nc.sync.dma_start(out=dst[:].bitcast(I32), in_=words.rearrange("e s p n -> p (e s) n").bitcast(I32))
+            nc.sync.dma_start(out=dst.bitcast(I32), in_=words.rearrange("e s p n -> p (e s) n").bitcast(I32))
 
         def merged(scales):
             return scales.rearrange("e s b n -> (e s) b n")
 
-        zero(zs, nc.vector)
+        zero(zs, nc.gpsimd)
         zero(wzs, nc.vector)
         zero(xs, nc.vector)
-        zero(w1s, nc.vector)
         nc.vector.memset(warm_in[:], 0.0)
         nc.scalar.activation(warm_out[:], warm_in[:], GELU)
-        zero(w2s, nc.gpsimd)
-        load_scales(w2s, merged(w2_scales), nc.gpsimd)
+        zero(w1s, nc.vector)
+        zero(w2s, nc.vector)
         make_identity(nc, ident[:])
+        load_scales(w1s, merged(w1_scales), nc.gpsimd)
         nc.vector.memset(out_z[:], 0.0)
         nc.vector.memset(out_x[:], 0.0)
 
         nc.sync.dma_start(list_z[:], offs2)
-        load_words(zw[0], z_words[0])
         load_scales(zs, z_scales, nc.sync)
+        load_words(zw[0], z_words[0])
         load_words(zw[1], z_words[1])
-        load_weights(wz, wz_words)
+        load_weights(wz[:, 0:2, :], wz_words[0:1])
         load_scales(wzs, merged(wz_scales), nc.sync)
         nc.sync.dma_start(list_x[:], offs)
         load_words(xw[0], x_words[0])
+        load_weights(wz[:, 2:4, :], wz_words[1:2])
         load_scales(xs, x_scales, nc.sync)
-        load_weights(w1, w1_words)
-        load_scales(w1s, merged(w1_scales), nc.sync)
-        load_weights(w2, w2_words)
+        load_weights(w1[:], w1_words)
+        load_weights(w2[:], w2_words)
+        load_scales(w2s, merged(w2_scales), nc.sync)
         nc.sync.dma_start(out=g2[:], in_=gate2)
         nc.sync.dma_start(out=g1[:], in_=gate1)
 
@@ -98,7 +99,7 @@ def tile_moe_mmo_gelu_kernel(tc, x_words, x_scales, z_words, z_scales, w1_words,
             "x": (list_x, xw, xs, w1, w1s, g1, out_x),
         }
         units = [("z", 0), ("z", 1), ("x", 0), ("x", 1)]
-        words, scales, grouped, sums, gated = {}, {}, {}, {}, {}
+        words, scales, hidden, grouped, sums, gated = {}, {}, {}, {}, {}, {}
 
         def offsets(u):
             side, e = units[u]
@@ -112,34 +113,33 @@ def tile_moe_mmo_gelu_kernel(tc, x_words, x_scales, z_words, z_scales, w1_words,
             scales[u, s] = tile([P, C], U8, "gs%d_%d" % (u, s))
             nc.vector.tensor_copy(scales[u, s][:], sides[units[u][0]][2][:, s, :].indirect(offsets(u)))
 
-        def first_layer(u):
+        def first_layer(u, j):
             side, e = units[u]
             w, ws = sides[side][3], sides[side][4]
             passes = len(sides[side][1])
-            turned = pst.tile([P, 4, P], F32, name="turned")
-            hs = []
-            for j in range(2):
-                cols = slice(j * P, (j + 1) * P)
-                acc = ps1.tile([P, H], F32, name="acc")
-                for s in range(passes):
-                    nc.tensor.matmul_mx(
-                        out=acc[:],
-                        lhsT=words[u, s][:, cols].bitcast(FP8X4),
-                        lhsT_scale=scales[u, s][:, cols],
-                        rhs=w[:, e * passes + s, :].bitcast(FP4X4),
-                        rhs_scale=ws[:, e * passes + s, :],
-                        start=(s == 0),
-                        stop=(s == passes - 1),
-                    )
-                h = tile([P, H], BF16, "h%d_%d" % (u, j))
-                nc.scalar.activation(
-                    h[:].rearrange("s (v q b) -> s v q b", v=2, b=2),
-                    acc[:].rearrange("s (q v b) -> s v q b", v=2, b=2),
-                    GELU,
+            cols = slice(j * P, (j + 1) * P)
+            acc = ps1.tile([P, H], F32, name="acc")
+            for s in range(passes):
+                nc.tensor.matmul_mx(
+                    out=acc[:],
+                    lhsT=words[u, s][:, cols].bitcast(FP8X4),
+                    lhsT_scale=scales[u, s][:, cols],
+                    rhs=w[:, e * passes + s, :].bitcast(FP4X4),
+                    rhs_scale=ws[:, e * passes + s, :],
+                    start=(s == 0),
+                    stop=(s == passes - 1),
                 )
-                hs.append(h)
+            hidden[u, j] = tile([P, H], BF16, "h%d_%d" % (u, j))
+            nc.scalar.activation(
+                hidden[u, j][:].rearrange("s (v q b) -> s v q b", v=2, b=2),
+                acc[:].rearrange("s (q v b) -> s v q b", v=2, b=2),
+                GELU,
+            )
+
+        def turn(u):
+            turned = pst.tile([P, 4, P], F32, name="turned")
             for j in range(2):
-                pairs = hs[j][:].bitcast(F32)
+                pairs = hidden[u, j][:].bitcast(F32)
                 for v in range(2):
                     nc.tensor.transpose(turned[:, 2 * j + v, :], pairs[:, v * P : (v + 1) * P], ident[:])
             grouped[u] = tile([P, 4 * C], BF16, "grouped%d" % u)
@@ -172,21 +172,29 @@ def tile_moe_mmo_gelu_kernel(tc, x_words, x_scales, z_words, z_scales, w1_words,
         def scatter(u):
             nc.vector.tensor_copy(sides[units[u][0]][6][:].indirect(offsets(u)), gated[u][:])
 
-        for u in range(2):
-            gather_words(u, 0)
-            gather_scales(u, 0)
-            gather_scales(u, 1)
-            gather_words(u, 1)
-            first_layer(u)
+        gather_scales(0, 0)
+        gather_scales(0, 1)
+        gather_words(0, 0)
+        gather_scales(1, 0)
+        gather_words(0, 1)
+        gather_scales(1, 1)
+        gather_words(1, 0)
+        gather_words(1, 1)
         gather_words(2, 0)
         gather_scales(2, 0)
-        first_layer(2)
         gather_words(3, 0)
+        first_layer(0, 0)
+        first_layer(0, 1)
+        first_layer(1, 0)
+        turn(0)
         second_layer(0)
         gather_scales(3, 0)
-        first_layer(3)
         gate(0)
         for u in range(1, 4):
+            first_layer(u, 1)
+            if u < 3:
+                first_layer(u + 1, 0)
+            turn(u)
             second_layer(u)
             scatter(u - 1)
             if u == 2:

@@ -12,6 +12,7 @@ U8 = mybir.dt.uint8
 FP8X4 = mybir.dt.float8_e4m3fn_x4
 FP4X4 = mybir.dt.float4_e2m1fn_x4
 GELU = mybir.ActivationFunctionType.Gelu_apprx_tanh
+COPY = mybir.ActivationFunctionType.Copy
 MULT = mybir.AluOpType.mult
 
 P = 128
@@ -23,9 +24,7 @@ def tile_moe_mmo_gelu_kernel(tc, x_words, x_scales, z_words, z_scales, w1_words,
     nc = tc.nc
     with ExitStack() as ctx:
         keep = ctx.enter_context(tc.tile_pool(name="keep", bufs=1))
-        ps1 = ctx.enter_context(tc.psum_pool(name="ps1", bufs=4))
-        pst = ctx.enter_context(tc.psum_pool(name="pst", bufs=2))
-        ps2 = ctx.enter_context(tc.psum_pool(name="ps2", bufs=2))
+        psum = ctx.enter_context(tc.psum_pool(name="psum", bufs=1))
 
         def tile(shape, dtype, name):
             return keep.tile(shape, dtype, name=name, align_bytes=64)
@@ -53,9 +52,9 @@ def tile_moe_mmo_gelu_kernel(tc, x_words, x_scales, z_words, z_scales, w1_words,
         def zero(plane, eng):
             eng.memset(plane[:].rearrange("p a n -> p (a n)").bitcast(I32), 0)
 
-        def load_scales(plane, rows, eng):
-            for r in range(4):
-                eng.dma_start(out=plane[r:P:32, :, :].bitcast(I32), in_=rows[:, r:16:4, :].rearrange("a q n -> q a n").bitcast(I32))
+        def load_scales(plane, rows, which=range(4)):
+            for r in which:
+                nc.sync.dma_start(out=plane[r:P:32, :, :].bitcast(I32), in_=rows[:, r:16:4, :].rearrange("a q n -> q a n").bitcast(I32))
 
         def load_words(dst, words):
             nc.sync.dma_start(out=dst[:], in_=words.rearrange("p t d -> p (t d)").bitcast(I32))
@@ -66,64 +65,69 @@ def tile_moe_mmo_gelu_kernel(tc, x_words, x_scales, z_words, z_scales, w1_words,
         def merged(scales):
             return scales.rearrange("e s b n -> (e s) b n")
 
-        zero(zs, nc.gpsimd)
-        zero(wzs, nc.vector)
-        zero(xs, nc.vector)
-        nc.vector.memset(warm_in[:], 0.0)
-        nc.scalar.activation(warm_out[:], warm_in[:], GELU)
-        zero(w1s, nc.vector)
-        zero(w2s, nc.vector)
+        zero(xs, nc.gpsimd)
         make_identity(nc, ident[:])
-        load_scales(w1s, merged(w1_scales), nc.gpsimd)
-        nc.vector.memset(out_z[:], 0.0)
-        nc.vector.memset(out_x[:], 0.0)
+        nc.vector.memset(warm_in[:], 0.0)
+        zero(w1s, nc.vector)
+        zero(zs, nc.vector)
+        zero(w2s, nc.vector)
+        zero(wzs, nc.vector)
+        nc.scalar.activation(warm_out[:], warm_in[:], GELU)
+        nc.scalar.activation(out_x[:], warm_in[:, 0:1].to_broadcast([P, T]), COPY)
+        nc.scalar.activation(out_z[:], warm_in[:, 0:1].to_broadcast([P, Q]), COPY)
 
-        nc.sync.dma_start(list_z[:], offs2)
-        load_scales(zs, z_scales, nc.sync)
-        load_words(zw[0], z_words[0])
-        load_words(zw[1], z_words[1])
-        load_weights(wz[:, 0:2, :], wz_words[0:1])
-        load_scales(wzs, merged(wz_scales), nc.sync)
+        w2_rows, wz_rows = merged(w2_scales), merged(wz_scales)
         nc.sync.dma_start(list_x[:], offs)
+        load_scales(xs, x_scales)
+        nc.sync.dma_start(list_z[:], offs2)
         load_words(xw[0], x_words[0])
-        load_weights(wz[:, 2:4, :], wz_words[1:2])
-        load_scales(xs, x_scales, nc.sync)
+        load_words(zw[0], z_words[0])
+        load_scales(w1s, merged(w1_scales))
         load_weights(w1[:], w1_words)
+        load_words(zw[1], z_words[1])
         load_weights(w2[:], w2_words)
-        load_scales(w2s, merged(w2_scales), nc.sync)
-        nc.sync.dma_start(out=g2[:], in_=gate2)
+        load_scales(zs, z_scales)
+        load_weights(wz[:], wz_words)
+        load_scales(wzs, wz_rows, [0])
         nc.sync.dma_start(out=g1[:], in_=gate1)
+        load_scales(wzs, wz_rows, [1])
+        load_scales(w2s, w2_rows, [0])
+        load_scales(wzs, wz_rows, [2])
+        load_scales(w2s, w2_rows, [1])
+        load_scales(wzs, wz_rows, [3])
+        load_scales(w2s, w2_rows, [2, 3])
+        nc.sync.dma_start(out=g2[:], in_=gate2)
 
         sides = {
             "z": (list_z, zw, zs, wz, wzs, g2, out_z),
             "x": (list_x, xw, xs, w1, w1s, g1, out_x),
         }
-        units = [("z", 0), ("z", 1), ("x", 0), ("x", 1)]
-        words, scales, hidden, grouped, sums, gated = {}, {}, {}, {}, {}, {}
+        units = [("x", 0), ("x", 1), ("z", 0), ("z", 1)]
+        planes, words, scales, hidden, grouped, sums, gated = {}, {}, {}, {}, {}, {}, {}
 
         def offsets(u):
             side, e = units[u]
             return sides[side][0][:, 16 * e : 16 * (e + 1)]
 
-        def gather_words(u, s):
-            words[u, s] = tile([P, C], U32, "gw%d_%d" % (u, s))
-            nc.vector.tensor_copy(words[u, s][:], sides[units[u][0]][1][s][:].bitcast(U32).indirect(offsets(u)))
+        def gather_words(side, s):
+            words[side, s] = tile([P, E * C], U32, "gw%s%d" % (side, s))
+            nc.vector.tensor_copy(words[side, s][:], sides[side][1][s][:].bitcast(U32).indirect(sides[side][0][:]))
 
-        def gather_scales(u, s):
-            scales[u, s] = tile([P, C], U8, "gs%d_%d" % (u, s))
-            nc.vector.tensor_copy(scales[u, s][:], sides[units[u][0]][2][:, s, :].indirect(offsets(u)))
+        def gather_scales(side, s):
+            scales[side, s] = tile([P, E * C], U8, "gs%s%d" % (side, s))
+            nc.vector.tensor_copy(scales[side, s][:], sides[side][2][:, s, :].indirect(sides[side][0][:]))
 
         def first_layer(u, j):
             side, e = units[u]
             w, ws = sides[side][3], sides[side][4]
             passes = len(sides[side][1])
-            cols = slice(j * P, (j + 1) * P)
-            acc = ps1.tile([P, H], F32, name="acc")
+            cols = slice(e * C + j * P, e * C + (j + 1) * P)
+            acc = psum.tile([P, H], F32, name="acc%d_%d" % (u, j), tag="first%d" % (2 * e + j))
             for s in range(passes):
                 nc.tensor.matmul_mx(
                     out=acc[:],
-                    lhsT=words[u, s][:, cols].bitcast(FP8X4),
-                    lhsT_scale=scales[u, s][:, cols],
+                    lhsT=words[side, s][:, cols].bitcast(FP8X4),
+                    lhsT_scale=scales[side, s][:, cols],
                     rhs=w[:, e * passes + s, :].bitcast(FP4X4),
                     rhs_scale=ws[:, e * passes + s, :],
                     start=(s == 0),
@@ -137,7 +141,7 @@ def tile_moe_mmo_gelu_kernel(tc, x_words, x_scales, z_words, z_scales, w1_words,
             )
 
         def turn(u):
-            turned = pst.tile([P, 4, P], F32, name="turned")
+            turned = psum.tile([P, 4, P], F32, name="turned%d" % u, tag="turned%d" % (u % 2))
             for j in range(2):
                 pairs = hidden[u, j][:].bitcast(F32)
                 for v in range(2):
@@ -149,17 +153,19 @@ def tile_moe_mmo_gelu_kernel(tc, x_words, x_scales, z_words, z_scales, w1_words,
             )
 
         def second_layer(u):
-            e = units[u][1]
-            codes = tile([P, C], U32, "codes%d" % u)
-            plane = tile([P, C], U8, "plane%d" % u)
-            nc.vector.quantize_mx(out=codes[:].bitcast(FP8X4), scales=plane[:], in_=grouped[u][:])
-            sums[u] = ps2.tile([P, C], F32, name="sums")
+            side, e = units[u]
+            codes = keep.tile([P, C], U32, name="codes%d" % u, tag="codes%d" % e, align_bytes=64)
+            if e == 0:
+                planes[side] = keep.tile([P, E, C], U8, name="plane" + side, tag="zs" if side == "x" else "planez", align_bytes=64)
+            plane = planes[side][:, e, :]
+            nc.vector.quantize_mx(out=codes[:].bitcast(FP8X4), scales=plane, in_=grouped[u][:])
+            sums[u] = psum.tile([P, C], F32, name="sums%d" % u, tag=["second0", "second1", "first3", "second0"][u])
             nc.tensor.matmul_mx(
                 out=sums[u][:],
                 lhsT=w2[:, e, :].bitcast(FP4X4),
                 lhsT_scale=w2s[:, e, :],
                 rhs=codes[:].bitcast(FP8X4),
-                rhs_scale=plane[:],
+                rhs_scale=plane,
                 start=True,
                 stop=True,
             )
@@ -172,33 +178,32 @@ def tile_moe_mmo_gelu_kernel(tc, x_words, x_scales, z_words, z_scales, w1_words,
         def scatter(u):
             nc.vector.tensor_copy(sides[units[u][0]][6][:].indirect(offsets(u)), gated[u][:])
 
-        gather_scales(0, 0)
-        gather_scales(0, 1)
-        gather_words(0, 0)
-        gather_scales(1, 0)
-        gather_words(0, 1)
-        gather_scales(1, 1)
-        gather_words(1, 0)
-        gather_words(1, 1)
-        gather_words(2, 0)
-        gather_scales(2, 0)
-        gather_words(3, 0)
-        first_layer(0, 0)
-        first_layer(0, 1)
-        first_layer(1, 0)
-        turn(0)
+        gather_scales("x", 0)
+        gather_words("x", 0)
+        gather_words("z", 0)
+        gather_words("z", 1)
+        gather_scales("z", 0)
+        gather_scales("z", 1)
+        def hidden_values(side_units):
+            for u in side_units:
+                first_layer(u, 0)
+                first_layer(u, 1)
+            for u in side_units:
+                turn(u)
+
+        hidden_values([0, 1])
         second_layer(0)
-        gather_scales(3, 0)
         gate(0)
-        for u in range(1, 4):
-            first_layer(u, 1)
-            if u < 3:
-                first_layer(u + 1, 0)
-            turn(u)
-            second_layer(u)
-            scatter(u - 1)
-            if u == 2:
-                nc.sync.dma_start(out=out[:, T:], in_=out_z[:])
-            gate(u)
-        scatter(3)
+        second_layer(1)
+        hidden_values([2, 3])
+        scatter(0)
+        gate(1)
+        second_layer(2)
+        scatter(1)
         nc.sync.dma_start(out=out[:, :T], in_=out_x[:])
+        gate(2)
+        second_layer(3)
+        scatter(2)
+        gate(3)
+        scatter(3)
+        nc.sync.dma_start(out=out[:, T:], in_=out_z[:])

@@ -52,9 +52,9 @@ def tile_moe_mmo_gelu_kernel(tc, x_words, x_scales, z_words, z_scales, w1_words,
         def zero(plane, eng):
             eng.memset(plane[:].rearrange("p a n -> p (a n)").bitcast(I32), 0)
 
-        def load_scales(plane, rows, which=range(4)):
+        def load_scales(plane, rows, which=range(4), queue=nc.sync):
             for r in which:
-                nc.sync.dma_start(out=plane[r:P:32, :, :].bitcast(I32), in_=rows[:, r:16:4, :].rearrange("a q n -> q a n").bitcast(I32))
+                queue.dma_start(out=plane[r:P:32, :, :].bitcast(I32), in_=rows[:, r:16:4, :].rearrange("a q n -> q a n").bitcast(I32))
 
         def load_words(dst, words):
             nc.sync.dma_start(out=dst[:], in_=words.rearrange("p t d -> p (t d)").bitcast(I32))
@@ -66,36 +66,31 @@ def tile_moe_mmo_gelu_kernel(tc, x_words, x_scales, z_words, z_scales, w1_words,
             return scales.rearrange("e s b n -> (e s) b n")
 
         zero(xs, nc.gpsimd)
+        zero(w2s, nc.gpsimd)
         make_identity(nc, ident[:])
+        load_scales(w2s, merged(w2_scales), queue=nc.gpsimd)
         nc.vector.memset(warm_in[:], 0.0)
         zero(w1s, nc.vector)
         zero(zs, nc.vector)
-        zero(w2s, nc.vector)
         zero(wzs, nc.vector)
         nc.scalar.activation(warm_out[:], warm_in[:], GELU)
         nc.scalar.activation(out_x[:], warm_in[:, 0:1].to_broadcast([P, T]), COPY)
         nc.scalar.activation(out_z[:], warm_in[:, 0:1].to_broadcast([P, Q]), COPY)
 
-        w2_rows, wz_rows = merged(w2_scales), merged(wz_scales)
         nc.sync.dma_start(list_x[:], offs)
-        load_scales(xs, x_scales)
         nc.sync.dma_start(list_z[:], offs2)
+        load_scales(xs, x_scales)
         load_words(xw[0], x_words[0])
-        load_words(zw[0], z_words[0])
-        load_scales(w1s, merged(w1_scales))
         load_weights(w1[:], w1_words)
-        load_words(zw[1], z_words[1])
-        load_weights(w2[:], w2_words)
+        load_scales(w1s, merged(w1_scales), [0, 1])
+        load_words(zw[0], z_words[0])
+        load_scales(w1s, merged(w1_scales), [2, 3])
         load_scales(zs, z_scales)
         load_weights(wz[:], wz_words)
-        load_scales(wzs, wz_rows, [0])
+        load_scales(wzs, merged(wz_scales))
+        load_weights(w2[:], w2_words)
+        load_words(zw[1], z_words[1])
         nc.sync.dma_start(out=g1[:], in_=gate1)
-        load_scales(wzs, wz_rows, [1])
-        load_scales(w2s, w2_rows, [0])
-        load_scales(wzs, wz_rows, [2])
-        load_scales(w2s, w2_rows, [1])
-        load_scales(wzs, wz_rows, [3])
-        load_scales(w2s, w2_rows, [2, 3])
         nc.sync.dma_start(out=g2[:], in_=gate2)
 
         sides = {
@@ -103,36 +98,43 @@ def tile_moe_mmo_gelu_kernel(tc, x_words, x_scales, z_words, z_scales, w1_words,
             "x": (list_x, xw, xs, w1, w1s, g1, out_x),
         }
         units = [("x", 0), ("x", 1), ("z", 0), ("z", 1)]
-        planes, words, scales, hidden, grouped, sums, gated = {}, {}, {}, {}, {}, {}, {}
+        pre, planes, words, scales, hidden, grouped, sums, gated = {}, {}, {}, {}, {}, {}, {}, {}
 
         def offsets(u):
             side, e = units[u]
             return sides[side][0][:, 16 * e : 16 * (e + 1)]
 
-        def gather_words(side, s):
+        def gather_words(side, s, pieces=1):
             words[side, s] = tile([P, E * C], U32, "gw%s%d" % (side, s))
-            nc.vector.tensor_copy(words[side, s][:], sides[side][1][s][:].bitcast(U32).indirect(sides[side][0][:]))
+            width = E * C // pieces
+            for a in range(0, E * C, width):
+                picks = sides[side][0][:, a // 16 : (a + width) // 16]
+                nc.vector.tensor_copy(words[side, s][:, a : a + width], sides[side][1][s][:].bitcast(U32).indirect(picks))
 
         def gather_scales(side, s):
             scales[side, s] = tile([P, E * C], U8, "gs%s%d" % (side, s))
             nc.vector.tensor_copy(scales[side, s][:], sides[side][2][:, s, :].indirect(sides[side][0][:]))
 
-        def first_layer(u, j):
+        def first_pass(u, j, s):
             side, e = units[u]
             w, ws = sides[side][3], sides[side][4]
             passes = len(sides[side][1])
             cols = slice(e * C + j * P, e * C + (j + 1) * P)
-            acc = psum.tile([P, H], F32, name="acc%d_%d" % (u, j), tag="first%d" % (2 * e + j))
-            for s in range(passes):
-                nc.tensor.matmul_mx(
-                    out=acc[:],
-                    lhsT=words[side, s][:, cols].bitcast(FP8X4),
-                    lhsT_scale=scales[side, s][:, cols],
-                    rhs=w[:, e * passes + s, :].bitcast(FP4X4),
-                    rhs_scale=ws[:, e * passes + s, :],
-                    start=(s == 0),
-                    stop=(s == passes - 1),
-                )
+            if s == 0:
+                pre[u, j] = psum.tile([P, H], F32, name="acc%d_%d" % (u, j), tag="first%d" % (2 * e + j))
+            nc.tensor.matmul_mx(
+                out=pre[u, j][:],
+                lhsT=words[side, s][:, cols].bitcast(FP8X4),
+                lhsT_scale=scales[side, s][:, cols],
+                rhs=w[:, e * passes + s, :].bitcast(FP4X4),
+                rhs_scale=ws[:, e * passes + s, :],
+                start=(s == 0),
+                stop=(s == passes - 1),
+            )
+
+        def first_layer(u, j):
+            first_pass(u, j, len(sides[units[u][0]][1]) - 1)
+            acc = pre[u, j]
             hidden[u, j] = tile([P, H], BF16, "h%d_%d" % (u, j))
             nc.scalar.activation(
                 hidden[u, j][:].rearrange("s (v q b) -> s v q b", v=2, b=2),
@@ -154,7 +156,7 @@ def tile_moe_mmo_gelu_kernel(tc, x_words, x_scales, z_words, z_scales, w1_words,
 
         def second_layer(u):
             side, e = units[u]
-            codes = keep.tile([P, C], U32, name="codes%d" % u, tag="codes%d" % e, align_bytes=64)
+            codes = keep.tile([P, C], U32, name="codes%d" % u, tag=["codes0", "zw1", "staged0", "codes0"][u], align_bytes=64)
             if e == 0:
                 planes[side] = keep.tile([P, E, C], U8, name="plane" + side, tag="zs" if side == "x" else "planez", align_bytes=64)
             plane = planes[side][:, e, :]
@@ -169,41 +171,41 @@ def tile_moe_mmo_gelu_kernel(tc, x_words, x_scales, z_words, z_scales, w1_words,
                 start=True,
                 stop=True,
             )
-
-        def gate(u):
-            side, e = units[u]
-            gated[u] = tile([P, C], F32, "gated%d" % u)
-            nc.vector.tensor_tensor(gated[u][:], sums[u][:], sides[side][5][:, e * C : (e + 1) * C], MULT)
+            gated[u] = tile([P, C], F32, "staged%d" % u)
+            nc.scalar.copy(gated[u][:], sums[u][:])
 
         def scatter(u):
-            nc.vector.tensor_copy(sides[units[u][0]][6][:].indirect(offsets(u)), gated[u][:])
+            side, e = units[u]
+            nc.vector.tensor_tensor(sides[side][6][:].indirect(offsets(u)), gated[u][:], sides[side][5][:, e * C : (e + 1) * C], MULT)
 
         gather_scales("x", 0)
         gather_words("x", 0)
         gather_words("z", 0)
-        gather_words("z", 1)
         gather_scales("z", 0)
         gather_scales("z", 1)
-        def hidden_values(side_units):
-            for u in side_units:
-                first_layer(u, 0)
-                first_layer(u, 1)
-            for u in side_units:
-                turn(u)
-
-        hidden_values([0, 1])
+        first_layer(0, 0)
+        first_layer(0, 1)
+        first_layer(1, 0)
+        turn(0)
+        first_layer(1, 1)
+        turn(1)
         second_layer(0)
-        gate(0)
+        for u in (2, 3):
+            for j in range(2):
+                first_pass(u, j, 0)
+        gather_words("z", 1, pieces=2)
         second_layer(1)
-        hidden_values([2, 3])
+        first_layer(2, 0)
+        first_layer(2, 1)
+        first_layer(3, 0)
+        turn(2)
+        first_layer(3, 1)
+        turn(3)
         scatter(0)
-        gate(1)
         second_layer(2)
         scatter(1)
         nc.sync.dma_start(out=out[:, :T], in_=out_x[:])
-        gate(2)
         second_layer(3)
         scatter(2)
-        gate(3)
         scatter(3)
         nc.sync.dma_start(out=out[:, T:], in_=out_z[:])

@@ -171,7 +171,9 @@ def tile_moe_mmo_gelu_kernel(tc, x_words, x_scales, z_words, z_scales, w1_words,
                 start=True,
                 stop=True,
             )
-            gated[u] = tile([P, C], F32, "staged%d" % u)
+
+        def evacuate(u):
+            gated[u] = keep.tile([P, C], F32, name="staged%d" % u, tag="h2_1" if u == 1 else "staged%d" % u, align_bytes=64)
             nc.scalar.copy(gated[u][:], sums[u][:])
 
         def scatter(u):
@@ -190,6 +192,7 @@ def tile_moe_mmo_gelu_kernel(tc, x_words, x_scales, z_words, z_scales, w1_words,
         first_layer(1, 1)
         turn(1)
         second_layer(0)
+        evacuate(0)
         for u in (2, 3):
             for j in range(2):
                 first_pass(u, j, 0)
@@ -199,13 +202,16 @@ def tile_moe_mmo_gelu_kernel(tc, x_words, x_scales, z_words, z_scales, w1_words,
         first_layer(2, 1)
         first_layer(3, 0)
         turn(2)
+        evacuate(1)
         first_layer(3, 1)
         turn(3)
         scatter(0)
         second_layer(2)
+        evacuate(2)
         scatter(1)
         nc.sync.dma_start(out=out[:, :T], in_=out_x[:])
         second_layer(3)
+        evacuate(3)
         scatter(2)
         scatter(3)
         nc.sync.dma_start(out=out[:, T:], in_=out_z[:])

from contextlib import ExitStack

import concourse.mybir as mybir
from concourse.masks import make_identity

F32 = mybir.dt.float32
BF16 = mybir.dt.bfloat16
I32 = mybir.dt.int32
U32 = mybir.dt.uint32
U16 = mybir.dt.uint16
U8 = mybir.dt.uint8
FP8X4 = mybir.dt.float8_e4m3fn_x4
FP4X4 = mybir.dt.float4_e2m1fn_x4
GELU = mybir.ActivationFunctionType.Gelu_apprx_tanh
COPY = mybir.ActivationFunctionType.Copy
MULT = mybir.AluOpType.mult

P = 128
T, Q, E, C, H, N = 768, 1024, 2, 256, 512, 128
FLOPS = 939524096


def tile_moe_mmo_gelu_kernel(tc, x_words, x_scales, z_words, z_scales, w1_words, w1_scales, wz_words, wz_scales, w2_words, w2_scales, gate1, gate2, offs, offs2, out):
    nc = tc.nc
    with ExitStack() as ctx:
        keep = ctx.enter_context(tc.tile_pool(name="keep", bufs=1))
        psum = ctx.enter_context(tc.psum_pool(name="psum", bufs=1))

        def tile(shape, dtype, name):
            return keep.tile(shape, dtype, name=name, align_bytes=64)

        list_x = keep.tile([P, E * C // 16], U16, name="list_x")
        list_z = keep.tile([P, E * C // 16], U16, name="list_z")
        xw = [tile([P, T], I32, "xw0")]
        zw = [tile([P, Q], I32, "zw%d" % s) for s in range(2)]
        xs = tile([P, 1, T], U8, "xs")
        zs = tile([P, 2, Q], U8, "zs")
        w1 = tile([P, 2, 2 * H], U8, "w1")
        wz = tile([P, 4, 2 * H], U8, "wz")
        w2 = tile([P, 2, 2 * N], U8, "w2")
        w1s = tile([P, 2, H], U8, "w1s")
        wzs = tile([P, 4, H], U8, "wzs")
        w2s = tile([P, 2, N], U8, "w2s")
        g1 = tile([P, E * C], F32, "g1")
        g2 = tile([P, E * C], F32, "g2")
        out_x = tile([P, T], F32, "out_x")
        out_z = tile([P, Q], F32, "out_z")
        ident = tile([P, P], F32, "ident")
        warm_in = tile([P, 8], F32, "warm_in")
        warm_out = tile([P, 8], F32, "warm_out")

        def zero(plane, eng):
            eng.memset(plane[:].rearrange("p a n -> p (a n)").bitcast(I32), 0)

        def load_scales(plane, rows, which=range(4), queue=nc.sync):
            for r in which:
                queue.dma_start(out=plane[r:P:32, :, :].bitcast(I32), in_=rows[:, r:16:4, :].rearrange("a q n -> q a n").bitcast(I32))

        def load_words(dst, words):
            nc.sync.dma_start(out=dst[:], in_=words.rearrange("p t d -> p (t d)").bitcast(I32))

        def load_weights(dst, words):
            nc.sync.dma_start(out=dst.bitcast(I32), in_=words.rearrange("e s p n -> p (e s) n").bitcast(I32))

        def merged(scales):
            return scales.rearrange("e s b n -> (e s) b n")

        zero(xs, nc.gpsimd)
        zero(w2s, nc.gpsimd)
        make_identity(nc, ident[:])
        load_scales(w2s, merged(w2_scales), queue=nc.gpsimd)
        nc.vector.memset(warm_in[:], 0.0)
        zero(w1s, nc.vector)
        zero(zs, nc.vector)
        zero(wzs, nc.vector)
        nc.scalar.activation(warm_out[:], warm_in[:], GELU)
        nc.scalar.activation(out_x[:], warm_in[:, 0:1].to_broadcast([P, T]), COPY)
        nc.scalar.activation(out_z[:], warm_in[:, 0:1].to_broadcast([P, Q]), COPY)

        nc.sync.dma_start(list_x[:], offs)
        nc.sync.dma_start(list_z[:], offs2)
        load_scales(xs, x_scales)
        load_words(xw[0], x_words[0])
        load_weights(w1[:], w1_words)
        load_scales(w1s, merged(w1_scales), [0, 1])
        load_words(zw[0], z_words[0])
        load_scales(w1s, merged(w1_scales), [2, 3])
        load_scales(zs, z_scales)
        load_weights(wz[:], wz_words)
        load_scales(wzs, merged(wz_scales))
        load_weights(w2[:], w2_words)
        load_words(zw[1], z_words[1])
        nc.sync.dma_start(out=g1[:], in_=gate1)
        nc.sync.dma_start(out=g2[:], in_=gate2)

        sides = {
            "z": (list_z, zw, zs, wz, wzs, g2, out_z),
            "x": (list_x, xw, xs, w1, w1s, g1, out_x),
        }
        units = [("x", 0), ("x", 1), ("z", 0), ("z", 1)]
        pre, planes, words, scales, hidden, grouped, sums, gated = {}, {}, {}, {}, {}, {}, {}, {}

        def offsets(u):
            side, e = units[u]
            return sides[side][0][:, 16 * e : 16 * (e + 1)]

        def gather_words(side, s, pieces=1):
            words[side, s] = tile([P, E * C], U32, "gw%s%d" % (side, s))
            width = E * C // pieces
            for a in range(0, E * C, width):
                picks = sides[side][0][:, a // 16 : (a + width) // 16]
                nc.vector.tensor_copy(words[side, s][:, a : a + width], sides[side][1][s][:].bitcast(U32).indirect(picks))

        def gather_scales(side, s):
            scales[side, s] = tile([P, E * C], U8, "gs%s%d" % (side, s))
            nc.vector.tensor_copy(scales[side, s][:], sides[side][2][:, s, :].indirect(sides[side][0][:]))

        def first_pass(u, j, s):
            side, e = units[u]
            w, ws = sides[side][3], sides[side][4]
            passes = len(sides[side][1])
            cols = slice(e * C + j * P, e * C + (j + 1) * P)
            if s == 0:
                pre[u, j] = psum.tile([P, H], F32, name="acc%d_%d" % (u, j), tag="first%d" % (2 * e + j))
            nc.tensor.matmul_mx(
                out=pre[u, j][:],
                lhsT=words[side, s][:, cols].bitcast(FP8X4),
                lhsT_scale=scales[side, s][:, cols],
                rhs=w[:, e * passes + s, :].bitcast(FP4X4),
                rhs_scale=ws[:, e * passes + s, :],
                start=(s == 0),
                stop=(s == passes - 1),
            )

        def first_layer(u, j):
            first_pass(u, j, len(sides[units[u][0]][1]) - 1)
            acc = pre[u, j]
            hidden[u, j] = tile([P, H], BF16, "h%d_%d" % (u, j))
            nc.scalar.activation(
                hidden[u, j][:].rearrange("s (v q b) -> s v q b", v=2, b=2),
                acc[:].rearrange("s (q v b) -> s v q b", v=2, b=2),
                GELU,
            )

        def turn(u):
            turned = psum.tile([P, 4, P], F32, name="turned%d" % u, tag="turned%d" % (u % 2))
            for j in range(2):
                pairs = hidden[u, j][:].bitcast(F32)
                for v in range(2):
                    nc.tensor.transpose(turned[:, 2 * j + v, :], pairs[:, v * P : (v + 1) * P], ident[:])
            grouped[u] = tile([P, 4 * C], BF16, "grouped%d" % u)
            nc.scalar.copy(
                grouped[u][:].bitcast(F32).rearrange("q (j s v) -> q j s v", j=2, v=2),
                turned[:].rearrange("q (j v) s -> q j s v", v=2),
            )

        def second_layer(u):
            side, e = units[u]
            codes = keep.tile([P, C], U32, name="codes%d" % u, tag=["codes0", "zw1", "staged0", "codes0"][u], align_bytes=64)
            if e == 0:
                planes[side] = keep.tile([P, E, C], U8, name="plane" + side, tag="zs" if side == "x" else "planez", align_bytes=64)
            plane = planes[side][:, e, :]
            nc.vector.quantize_mx(out=codes[:].bitcast(FP8X4), scales=plane, in_=grouped[u][:])
            sums[u] = psum.tile([P, C], F32, name="sums%d" % u, tag=["second0", "second1", "first3", "second0"][u])
            nc.tensor.matmul_mx(
                out=sums[u][:],
                lhsT=w2[:, e, :].bitcast(FP4X4),
                lhsT_scale=w2s[:, e, :],
                rhs=codes[:].bitcast(FP8X4),
                rhs_scale=plane,
                start=True,
                stop=True,
            )

        def evacuate(u):
            gated[u] = keep.tile([P, C], F32, name="staged%d" % u, tag="h2_1" if u == 1 else "staged%d" % u, align_bytes=64)
            nc.scalar.copy(gated[u][:], sums[u][:])

        def scatter(u):
            side, e = units[u]
            nc.vector.tensor_tensor(sides[side][6][:].indirect(offsets(u)), gated[u][:], sides[side][5][:, e * C : (e + 1) * C], MULT)

        gather_scales("x", 0)
        gather_words("x", 0)
        gather_words("z", 0)
        gather_scales("z", 0)
        gather_scales("z", 1)
        first_layer(0, 0)
        first_layer(0, 1)
        first_layer(1, 0)
        turn(0)
        first_layer(1, 1)
        turn(1)
        second_layer(0)
        evacuate(0)
        for u in (2, 3):
            for j in range(2):
                first_pass(u, j, 0)
        gather_words("z", 1, pieces=2)
        second_layer(1)
        first_layer(2, 0)
        first_layer(2, 1)
        first_layer(3, 0)
        turn(2)
        evacuate(1)
        first_layer(3, 1)
        turn(3)
        scatter(0)
        second_layer(2)
        evacuate(2)
        scatter(1)
        nc.sync.dma_start(out=out[:, :T], in_=out_x[:])
        second_layer(3)
        evacuate(3)
        scatter(2)
        scatter(3)
        nc.sync.dma_start(out=out[:, T:], in_=out_z[:])
